import numpy as np, ml_dtypes
CORES = [16,23,24,31,64,71]
N = 6
import mx_ref
NC, G, MB, ROOT = 128, 4, 2, 2
C = np.float32(0.043)
BF = ml_dtypes.bfloat16
def cut(t, i, w=512):
    return t[:, w * i:w * i + w]
def tile(rs):
    return np.stack(rs, axis=2).reshape(128, -1).astype(BF)
def layer(w, X):
    out = []
    for i in range(G):
        for t in range(len(X)):
            p = mx_ref.matmul(mx_ref.quantize(cut(w, len(X) * i + t)), X[t])
            z = p if t == 0 else z + p
        out.append(z)
    return out
def act(Z):
    return [np.maximum(z, 0) * C for z in Z]
def setup_inputs(rng):
    def f(*shape):
        return mx_ref.flush((rng.standard_normal(shape, dtype=np.float32) * np.exp2(rng.integers(-2, 3, shape[:-1] + (1,)))).astype(BF))
    return {"x": f(N, 128, MB * 4 * NC), "w1": f(N, 128, G * 512), "w2": f(N, 128, 512)}
def setup_inputs_blocks(rng):
    d = setup_inputs(rng)
    for k in ("x", "w1", "w2"): d[k] = mx_ref.spread(d[k], rng, 4)
    return d
def setup_inputs_wide(rng):
    d = setup_inputs(rng)
    for k in ("x", "w1", "w2"): d[k] = mx_ref.flush((d[k].astype(np.float32) * np.exp2(rng.integers(-8, 9, (N, 1, 1))).astype(np.float32)).astype(BF))
    return d
def setup_inputs_zeros(rng):
    d = setup_inputs(rng); v = d["x"].reshape(N, 128, -1, 4).copy()
    v[np.broadcast_to((rng.random((N, 1, v.shape[2], 1)) < 0.33), v.shape)] = 0
    d["x"] = v.reshape(d["x"].shape)
    return d
def reference(x, w1, w2):
    H = [mx_ref.quantize(tile(act(layer(w1[ROOT], [mx_ref.quantize(cut(x[ROOT], m, 4 * NC))])))) for m in range(MB)]
    y = np.zeros((N, 128, MB * NC), np.float32)
    for r in range(N):
        qw = mx_ref.quantize(w2[r])
        for m in range(MB):
            y[r][:, NC * m:NC * m + NC] = mx_ref.matmul(qw, H[m])
    return {"y": y}

@@ -1,0 +1,168 @@
+from concourse.bass import DstId, RemoteDMATransfer
+from concourse.mybir import dt, AluOpType, ActivationFunctionType
+
+NC, G, MB = 128, 4, 2
+W = NC * MB
+TW = 4 * NC
+C = 0.043
+SIM_CORES = 80
+
+SCRATCH = {
+    "x_in": ("sbuf", [128, MB * TW], "bfloat16"),
+    "w1_in": ("sbuf", [128, G * TW], "bfloat16"),
+    "w2_in": ("sbuf", [128, TW], "bfloat16"),
+    "xq": ("sbuf", [128, W], "float8_e4m3fn_x4"),
+    "xs": ("sbuf", [128, W], "uint8"),
+    "w1q": ("sbuf", [128, G * NC], "float8_e4m3fn_x4"),
+    "w1s": ("sbuf", [128, G * NC], "uint8"),
+    "w2q": ("sbuf", [128, NC], "float8_e4m3fn_x4"),
+    "w2s": ("sbuf", [128, NC], "uint8"),
+    "h": ("sbuf", [128, MB * TW], "bfloat16"),
+    "hq": ("sbuf", [128, W], "float8_e4m3fn_x4"),
+    "hs": ("sbuf", [128, W], "uint8"),
+    "ysb": ("sbuf", [128, W], "float32"),
+    "z": ("psum", [128, 512 * (G + 1)], "float32"),
+    "yp": ("psum", [128, 512 * MB], "float32"),
+}
+PIECES = [(k, lo, hi) for k in "cs" for lo, hi in ((0, NC), (NC, W), (0, W))]
+
+
+def piece_sem(p):
+    return "%s%d_%d" % p
+
+
+SEMAPHORES = (["lx", "lv", "qx", "qv", "act", "act_v", "qh", "sent", "ya", "yv", "sta", "stv"]
+              + ["lw%d" % i for i in range(G)] + ["qw%d" % i for i in range(G)]
+              + ["z%d" % i for i in range(G + 1)] + ["ym%d" % m for m in range(MB)]
+              + [piece_sem(p) for p in PIECES])
+
+
+def plan(T, topo):
+    root = T.cores[T.root]
+    far = [c for c in T.cores if c != root and not topo.may_write(root, c)]
+    near = [c for c in T.cores if c != root and topo.may_write(root, c)]
+    owners = [c for c in range(SIM_CORES) if c != root and topo.chip(c) == topo.chip(root)
+              and all(topo.may_write(c, d) for d in far)]
+    owners.sort(key=lambda c: (c not in near, c))
+    calls = {}
+    halves = ((0, NC), (NC, W))
+    to = [list(near), list(near)]
+    for die in sorted({topo.die(d) for d in far}):
+        mine = [c for c in owners if topo.die(c) == die]
+        dsts = [d for d in far if topo.die(d) == die]
+        dsts.sort(key=lambda d: topo.mates(topo.chip(d), topo.chip(root)))
+        for m in range(MB):
+            relay = mine[m]
+            if relay not in to[m]:
+                to[m].append(relay)
+            for k in "cs":
+                calls.setdefault(relay, []).append([((k,) + halves[m], dsts, slice(0, None, 2))])
+    calls[root] = [[((k,) + halves[m], to[m], slice(2 * m, None, 4)) for m in range(MB)] for k in "cs"]
+    return calls
+
+
+def view(T, p):
+    k, lo, hi = p
+    return T.hq[:, lo:hi].bitcast(dt.uint8) if k == "c" else T.hs[:, lo:hi]
+
+
+def engines(topo, src, dsts, pick):
+    m = topo.mask(src, dsts[0])
+    for d in dsts[1:]:
+        m &= topo.mask(src, d)
+    return [b for b in range(m.bit_length()) if m >> b & 1][pick]
+
+
+def rank_program(g, core, T, topo):
+    rank = T.rank_of(core)
+    calls = plan(T, topo)
+    S = T.sem
+    landing = {}
+    for src, cs in calls.items():
+        for call in cs:
+            for p, dsts, pick in call:
+                if core in dsts:
+                    landing[p] = len(engines(topo, src, dsts, pick))
+    root = rank == T.root
+
+    if root:
+        g.sync.dma_start(T.x_in[:], T.x[:]).then_inc(S.lx, 16)
+        for i in range(G):
+            q = g.sync if i % 2 else g.scalar
+            q.dma_start(T.w1_in[:, TW * i:TW * i + TW], T.w1[:, TW * i:TW * i + TW]).then_inc(S["lw%d" % i], 16)
+    if rank is not None:
+        (g.scalar if root else g.sync).dma_start(T.w2_in[:], T.w2[:]).then_inc(S.lv, 16)
+    if root:
+        g.vector.wait_ge(S.lx, 16)
+        g.vector.quantize_mx(T.xq[:], T.xs[:], T.x_in[:]).then_inc(S.qx, 1)
+        for i in range(G):
+            a, b = NC * i, NC * i + NC
+            g.vector.wait_ge(S["lw%d" % i], 16)
+            g.vector.quantize_mx(T.w1q[:, a:b], T.w1s[:, a:b], T.w1_in[:, TW * i:TW * i + TW]).then_inc(S["qw%d" % i], 1)
+        g.tensor.wait_ge(S.qx, 1)
+        for i in range(G):
+            a, b = NC * i, NC * i + NC
+            g.tensor.wait_ge(S["qw%d" % i], 1)
+            parts = [(0, W, i)] if i < G - 1 else [(NC * m, NC * m + NC, i + m) for m in range(MB)]
+            for lo, hi, bank in parts:
+                g.tensor.matmul_mx(T.z[:, 512 * bank:512 * bank + hi - lo], T.w1q[:, a:b], T.w1s[:, a:b],
+                                   T.xq[:, lo:hi], T.xs[:, lo:hi], True, True).then_inc(S["z%d" % bank], 1)
+        for i in range(G - 1):
+            g.scalar.wait_ge(S["z%d" % i], 1)
+            g.scalar.activation(T.h[:, i:MB * TW:G], T.z[:, 512 * i:512 * i + W], ActivationFunctionType.Relu,
+                                scale=C).then_inc(S.act, 1)
+        g.scalar.wait_ge(S["z%d" % (G - 1)], 1)
+        g.scalar.activation(T.h[:, G - 1:TW:G], T.z[:, 512 * (G - 1):512 * (G - 1) + NC],
+                            ActivationFunctionType.Relu, scale=C).then_inc(S.act, 1)
+        g.vector.wait_ge(S["z%d" % G], 1)
+        g.vector.tensor_scalar(T.h[:, TW + G - 1:2 * TW:G], T.z[:, 512 * G:512 * G + NC], 0.0, C,
+                               AluOpType.max, AluOpType.mult).then_inc(S.act_v, 1)
+        g.vector.wait_ge(S.act_v, 1)
+        g.vector.wait_ge(S.act, G)
+        g.vector.quantize_mx(T.hq[:], T.hs[:], T.h[:]).then_inc(S.qh, 1)
+    if rank is not None:
+        g.vector.wait_ge(S.lv, 16)
+        g.vector.quantize_mx(T.w2q[:], T.w2s[:], T.w2_in[:]).then_inc(S.qv, 1)
+
+    total = 0
+    if root:
+        g.wait_ge(S.qh, 1)
+    for call in calls.get(core, []):
+        trs, n = [], 0
+        for p, dsts, pick in call:
+            if not root:
+                g.wait_ge(S[piece_sem(p)], landing[p])
+            eng = engines(topo, core, dsts, pick)
+            n += len(eng)
+            ids = [DstId(rid=topo.addr(d)[0], pnc=topo.addr(d)[1]) for d in dsts]
+            trs.append(RemoteDMATransfer(dst_ids=ids, dma_engine_mask=sum(1 << b for b in eng),
+                                         remote_sem=S[piece_sem(p)], srcs=[view(T, p)],
+                                         dsts=[view(T, p) for d in dsts]))
+        g.remote_dma_fused(trs, local_sem=S.sent)
+        total += n
+    if total:
+        g.wait_ge(S.sent, total)
+
+    if rank is not None:
+        g.tensor.wait_ge(S.qv, 1)
+        if root:
+            g.tensor.wait_ge(S.qh, 1)
+        waited = set()
+        for m in range(MB):
+            a, b = NC * m, NC * m + NC
+            for p in sorted(landing):
+                if p not in waited and p[1] < b and p[2] > a:
+                    waited.add(p)
+                    g.tensor.wait_ge(S[piece_sem(p)], landing[p])
+            g.tensor.matmul_mx(T.yp[:, 512 * m:512 * m + NC], T.w2q[:], T.w2s[:], T.hq[:, a:b], T.hs[:, a:b],
+                               True, True).then_inc(S["ym%d" % m], 1)
+        g.scalar.wait_ge(S.ym0, 1)
+        g.scalar.activation(T.ysb[:, 0:NC], T.yp[:, 0:NC], ActivationFunctionType.Copy).then_inc(S.ya, 1)
+        g.scalar.wait_ge(S.ya, 1)
+        g.scalar.dma_start(T.y[:, 0:NC], T.ysb[:, 0:NC]).then_inc(S.sta, 16)
+        g.vector.wait_ge(S.ym1, 1)
+        g.vector.tensor_copy(T.ysb[:, NC:W], T.yp[:, 512:512 + NC]).then_inc(S.yv, 1)
+        g.sync.wait_ge(S.yv, 1)
+        g.sync.dma_start(T.y[:, NC:W], T.ysb[:, NC:W]).then_inc(S.stv, 16)
+        g.scalar.wait_ge(S.sta, 16)
+        g.sync.wait_ge(S.stv, 16)

@@ -21,19 +21,22 @@ SCRATCH = {
     "hq": ("sbuf", [128, W], "float8_e4m3fn_x4"),
     "hs": ("sbuf", [128, W], "uint8"),
     "ysb": ("sbuf", [128, W], "float32"),
-    "z": ("psum", [128, 512 * (G + 1)], "float32"),
+    "z": ("psum", [128, 512 * (G + 2)], "float32"),
     "yp": ("psum", [128, 512 * MB], "float32"),
 }
-PIECES = [(k, lo, hi) for k in "cs" for lo, hi in ((0, NC), (NC, W), (0, W))]
+C0, C1, SS = ("c", 0, NC), ("c", NC, W), ("s", 0, W)
+PIECES = [C0, C1, SS]
 
 
 def piece_sem(p):
     return "%s%d_%d" % p
 
 
-SEMAPHORES = (["lx", "lv", "qx", "qv", "act", "act_v", "qh", "sent", "ya", "yv", "sta", "stv"]
+SEMAPHORES = (["lv", "qv", "act0", "act1", "actv", "sent", "ya", "yv", "sta", "stv"]
+              + ["lx%d" % m for m in range(MB)] + ["qx%d" % m for m in range(MB)]
+              + ["qh%d" % m for m in range(MB)] + ["ym%d" % m for m in range(MB)]
               + ["lw%d" % i for i in range(G)] + ["qw%d" % i for i in range(G)]
-              + ["z%d" % i for i in range(G + 1)] + ["ym%d" % m for m in range(MB)]
+              + ["z%d_%d" % (i, m) for i in range(G) for m in range(MB)]
               + [piece_sem(p) for p in PIECES])
 
 
@@ -44,20 +47,15 @@ def plan(T, topo):
     owners = [c for c in range(SIM_CORES) if c != root and topo.chip(c) == topo.chip(root)
               and all(topo.may_write(c, d) for d in far)]
     owners.sort(key=lambda c: (c not in near, c))
-    calls = {}
-    halves = ((0, NC), (NC, W))
-    to = [list(near), list(near)]
+    calls, to = {}, list(near)
     for die in sorted({topo.die(d) for d in far}):
-        mine = [c for c in owners if topo.die(c) == die]
+        relay = [c for c in owners if topo.die(c) == die][0]
         dsts = [d for d in far if topo.die(d) == die]
         dsts.sort(key=lambda d: topo.mates(topo.chip(d), topo.chip(root)))
-        for m in range(MB):
-            relay = mine[m]
-            if relay not in to[m]:
-                to[m].append(relay)
-            for k in "cs":
-                calls.setdefault(relay, []).append([((k,) + halves[m], dsts, slice(0, None, 2))])
-    calls[root] = [[((k,) + halves[m], to[m], slice(2 * m, None, 4)) for m in range(MB)] for k in "cs"]
+        if relay not in to:
+            to.append(relay)
+        calls[relay] = [[(p, dsts, slice(0, None))] for p in PIECES]
+    calls[root] = [[(p, to, slice(0, None, 2))] for p in PIECES]
     return calls
 
 
@@ -85,73 +83,102 @@ def rank_program(g, core, T, topo):
                     landing[p] = len(engines(topo, src, dsts, pick))
     root = rank == T.root
 
+    def load_x(q, m):
+        q.dma_start(T.x_in[:, TW * m:TW * m + TW], T.x[:, TW * m:TW * m + TW]).then_inc(S["lx%d" % m], 16)
+
+    def load_w1(q, i):
+        q.dma_start(T.w1_in[:, TW * i:TW * i + TW], T.w1[:, TW * i:TW * i + TW]).then_inc(S["lw%d" % i], 16)
+
+    def quant_x(m):
+        g.vector.wait_ge(S["lx%d" % m], 16)
+        g.vector.quantize_mx(T.xq[:, NC * m:NC * m + NC], T.xs[:, NC * m:NC * m + NC],
+                             T.x_in[:, TW * m:TW * m + TW]).then_inc(S["qx%d" % m], 1)
+
+    def quant_h(m):
+        g.vector.quantize_mx(T.hq[:, NC * m:NC * m + NC], T.hs[:, NC * m:NC * m + NC],
+                             T.h[:, TW * m:TW * m + TW]).then_inc(S["qh%d" % m], 1)
+
+    def bank(i, m):
+        return 512 * (i if m == 0 else (G + i) % (G + 2))
+
+    def z(i, m):
+        return T.z[:, bank(i, m):bank(i, m) + NC]
+
+    def product(i, m):
+        a, b, c, d = NC * i, NC * i + NC, NC * m, NC * m + NC
+        g.tensor.matmul_mx(z(i, m), T.w1q[:, a:b], T.w1s[:, a:b], T.xq[:, c:d], T.xs[:, c:d],
+                           True, True).then_inc(S["z%d_%d" % (i, m)], 1)
+
+    def relu_scalar(i, m):
+        g.scalar.wait_ge(S["z%d_%d" % (i, m)], 1)
+        g.scalar.activation(T.h[:, TW * m + i:TW * m + TW:G], z(i, m), ActivationFunctionType.Relu,
+                            scale=C).then_inc(S["act%d" % m], 1)
+
+    def relu_vector(i, m):
+        g.vector.wait_ge(S["z%d_%d" % (i, m)], 1)
+        g.vector.tensor_scalar(T.h[:, TW * m + i:TW * m + TW:G], z(i, m), 0.0, C,
+                               AluOpType.max, AluOpType.mult).then_inc(S.actv, 1)
+
     if root:
-        g.sync.dma_start(T.x_in[:], T.x[:]).then_inc(S.lx, 16)
+        load_x(g.sync, 0)
         for i in range(G):
-            q = g.sync if i % 2 else g.scalar
-            q.dma_start(T.w1_in[:, TW * i:TW * i + TW], T.w1[:, TW * i:TW * i + TW]).then_inc(S["lw%d" % i], 16)
+            load_w1(g.sync if i % 2 else g.scalar, i)
+        load_x(g.scalar, 1)
     if rank is not None:
-        (g.scalar if root else g.sync).dma_start(T.w2_in[:], T.w2[:]).then_inc(S.lv, 16)
+        g.sync.dma_start(T.w2_in[:], T.w2[:]).then_inc(S.lv, 16)
     if root:
-        g.vector.wait_ge(S.lx, 16)
-        g.vector.quantize_mx(T.xq[:], T.xs[:], T.x_in[:]).then_inc(S.qx, 1)
+        quant_x(0)
+        g.tensor.wait_ge(S.qx0, 1)
         for i in range(G):
             a, b = NC * i, NC * i + NC
             g.vector.wait_ge(S["lw%d" % i], 16)
             g.vector.quantize_mx(T.w1q[:, a:b], T.w1s[:, a:b], T.w1_in[:, TW * i:TW * i + TW]).then_inc(S["qw%d" % i], 1)
-        g.tensor.wait_ge(S.qx, 1)
-        for i in range(G):
-            a, b = NC * i, NC * i + NC
             g.tensor.wait_ge(S["qw%d" % i], 1)
-            parts = [(0, W, i)] if i < G - 1 else [(NC * m, NC * m + NC, i + m) for m in range(MB)]
-            for lo, hi, bank in parts:
-                g.tensor.matmul_mx(T.z[:, 512 * bank:512 * bank + hi - lo], T.w1q[:, a:b], T.w1s[:, a:b],
-                                   T.xq[:, lo:hi], T.xs[:, lo:hi], True, True).then_inc(S["z%d" % bank], 1)
-        for i in range(G - 1):
-            g.scalar.wait_ge(S["z%d" % i], 1)
-            g.scalar.activation(T.h[:, i:MB * TW:G], T.z[:, 512 * i:512 * i + W], ActivationFunctionType.Relu,
-                                scale=C).then_inc(S.act, 1)
-        g.scalar.wait_ge(S["z%d" % (G - 1)], 1)
-        g.scalar.activation(T.h[:, G - 1:TW:G], T.z[:, 512 * (G - 1):512 * (G - 1) + NC],
-                            ActivationFunctionType.Relu, scale=C).then_inc(S.act, 1)
-        g.vector.wait_ge(S["z%d" % G], 1)
-        g.vector.tensor_scalar(T.h[:, TW + G - 1:2 * TW:G], T.z[:, 512 * G:512 * G + NC], 0.0, C,
-                               AluOpType.max, AluOpType.mult).then_inc(S.act_v, 1)
-        g.vector.wait_ge(S.act_v, 1)
-        g.vector.wait_ge(S.act, G)
-        g.vector.quantize_mx(T.hq[:], T.hs[:], T.h[:]).then_inc(S.qh, 1)
+            product(i, 0)
+            relu_scalar(i, 0)
+        g.vector.wait_ge(S.act0, G)
+        quant_h(0)
+        quant_x(1)
+        g.tensor.wait_ge(S.qx1, 1)
+        for i in range(G):
+            if i == 2:
+                g.tensor.wait_ge(S.act0, G)
+            product(i, 1)
+            (relu_vector if i % 2 else relu_scalar)(i, 1)
+        g.vector.wait_ge(S.act1, G // 2)
+        g.vector.wait_ge(S.actv, G // 2)
+        quant_h(1)
     if rank is not None:
         g.vector.wait_ge(S.lv, 16)
         g.vector.quantize_mx(T.w2q[:], T.w2s[:], T.w2_in[:]).then_inc(S.qv, 1)
 
     total = 0
-    if root:
-        g.wait_ge(S.qh, 1)
     for call in calls.get(core, []):
-        trs, n = [], 0
+        trs = []
         for p, dsts, pick in call:
-            if not root:
+            if root:
+                g.wait_ge(S.qh0 if p == C0 else S.qh1, 1)
+            else:
                 g.wait_ge(S[piece_sem(p)], landing[p])
             eng = engines(topo, core, dsts, pick)
-            n += len(eng)
+            total += len(eng)
             ids = [DstId(rid=topo.addr(d)[0], pnc=topo.addr(d)[1]) for d in dsts]
             trs.append(RemoteDMATransfer(dst_ids=ids, dma_engine_mask=sum(1 << b for b in eng),
                                          remote_sem=S[piece_sem(p)], srcs=[view(T, p)],
                                          dsts=[view(T, p) for d in dsts]))
         g.remote_dma_fused(trs, local_sem=S.sent)
-        total += n
     if total:
         g.wait_ge(S.sent, total)
 
     if rank is not None:
         g.tensor.wait_ge(S.qv, 1)
-        if root:
-            g.tensor.wait_ge(S.qh, 1)
         waited = set()
         for m in range(MB):
             a, b = NC * m, NC * m + NC
-            for p in sorted(landing):
-                if p not in waited and p[1] < b and p[2] > a:
+            if root:
+                g.tensor.wait_ge(S["qh%d" % m], 1)
+            for p in PIECES:
+                if p in landing and p not in waited and p[1] < b and p[2] > a:
                     waited.add(p)
                     g.tensor.wait_ge(S[piece_sem(p)], landing[p])
             g.tensor.matmul_mx(T.yp[:, 512 * m:512 * m + NC], T.w2q[:], T.w2s[:], T.hq[:, a:b], T.hs[:, a:b],

@@ -24,8 +24,10 @@ SCRATCH = {
     "z": ("psum", [128, 512 * (G + 2)], "float32"),
     "yp": ("psum", [128, 512 * MB], "float32"),
 }
-C0, C1, SS = ("c", 0, NC), ("c", NC, W), ("s", 0, W)
-PIECES = [C0, C1, SS]
+C0, C1, S0, S1 = ("c", 0, NC), ("c", NC, W), ("s", 0, NC), ("s", NC, W)
+PIECES = [S0, C0, S1, C1]
+BY_CHIP = (S0, C1)
+LOADS = [("x", 0), ("w1", 0), ("w1", 1), ("w1", 2), ("w1", 3), ("x", 1)]
 
 
 def piece_sem(p):
@@ -33,29 +35,45 @@ def piece_sem(p):
 
 
 SEMAPHORES = (["lv", "qv", "act0", "act1", "actv", "sent", "ya", "yv", "sta", "stv"]
-              + ["lx%d" % m for m in range(MB)] + ["qx%d" % m for m in range(MB)]
+              + ["l%s_%d" % l for l in LOADS] + ["qx%d" % m for m in range(MB)]
               + ["qh%d" % m for m in range(MB)] + ["ym%d" % m for m in range(MB)]
-              + ["lw%d" % i for i in range(G)] + ["qw%d" % i for i in range(G)]
+              + ["qw%d" % i for i in range(G)]
               + ["z%d_%d" % (i, m) for i in range(G) for m in range(MB)]
               + [piece_sem(p) for p in PIECES])
 
 
 def plan(T, topo):
     root = T.cores[T.root]
+    home = topo.chip(root)
     far = [c for c in T.cores if c != root and not topo.may_write(root, c)]
     near = [c for c in T.cores if c != root and topo.may_write(root, c)]
-    owners = [c for c in range(SIM_CORES) if c != root and topo.chip(c) == topo.chip(root)
+
+    def owners(ok):
+        cs = [c for c in range(SIM_CORES) if c != root and topo.may_write(root, c) and ok(topo.chip(c))
               and all(topo.may_write(c, d) for d in far)]
-    owners.sort(key=lambda c: (c not in near, c))
-    calls, to = {}, list(near)
+        return sorted(cs, key=lambda c: (c not in near, c))
+
+    by_die, by_chip = [], []
     for die in sorted({topo.die(d) for d in far}):
-        relay = [c for c in owners if topo.die(c) == die][0]
-        dsts = [d for d in far if topo.die(d) == die]
-        dsts.sort(key=lambda d: topo.mates(topo.chip(d), topo.chip(root)))
-        if relay not in to:
-            to.append(relay)
-        calls[relay] = [[(p, dsts, slice(0, None))] for p in PIECES]
-    calls[root] = [[(p, to, slice(0, None, 2))] for p in PIECES]
+        relay = [c for c in owners(lambda k: k == home) if topo.die(c) == die][0]
+        ranks = [d for d in far if topo.die(d) == die]
+        ranks.sort(key=lambda d: topo.mates(topo.chip(d), home))
+        by_die.append((relay, ranks))
+    taken = [r for r, ranks in by_die]
+    for chip in sorted({topo.chip(d) for d in far}, key=lambda k: topo.mates(k, home)):
+        free = [c for c in owners(lambda k: topo.mates(k, chip)) if c not in taken]
+        want = topo.die(near[0]) if topo.mates(chip, home) else topo.die(root)
+        by_chip.append(([c for c in free if topo.die(c) == want][0], [d for d in far if topo.chip(d) == chip]))
+    calls = {root: []}
+    for p in PIECES:
+        relays = by_chip if p in BY_CHIP else by_die
+        calls[root].append((p, [r for r, ranks in relays]))
+        for r, ranks in relays:
+            calls.setdefault(r, []).append((p, ranks))
+    for p in PIECES:
+        rest = [c for c in near if all(c not in dsts for q, dsts in calls[root] if q == p)]
+        if rest:
+            calls[root].append((p, rest))
     return calls
 
 
@@ -64,35 +82,37 @@ def view(T, p):
     return T.hq[:, lo:hi].bitcast(dt.uint8) if k == "c" else T.hs[:, lo:hi]
 
 
-def engines(topo, src, dsts, pick):
-    m = topo.mask(src, dsts[0])
-    for d in dsts[1:]:
-        m &= topo.mask(src, d)
-    return [b for b in range(m.bit_length()) if m >> b & 1][pick]
+def engine_mask(topo, src, cs):
+    m = -1
+    for p, dsts in cs:
+        for d in dsts:
+            m &= topo.mask(src, d)
+    return m
 
 
 def rank_program(g, core, T, topo):
     rank = T.rank_of(core)
     calls = plan(T, topo)
     S = T.sem
-    landing = {}
-    for src, cs in calls.items():
-        for call in cs:
-            for p, dsts, pick in call:
-                if core in dsts:
-                    landing[p] = len(engines(topo, src, dsts, pick))
+    landing = {p: engine_mask(topo, src, cs).bit_count()
+               for src, cs in calls.items() for p, dsts in cs if core in dsts}
     root = rank == T.root
 
-    def load_x(q, m):
-        q.dma_start(T.x_in[:, TW * m:TW * m + TW], T.x[:, TW * m:TW * m + TW]).then_inc(S["lx%d" % m], 16)
-
-    def load_w1(q, i):
-        q.dma_start(T.w1_in[:, TW * i:TW * i + TW], T.w1[:, TW * i:TW * i + TW]).then_inc(S["lw%d" % i], 16)
+    def load(k):
+        what, i = LOADS[k]
+        q = g.scalar if k % 2 else g.sync
+        src, dst = (T.x, T.x_in) if what == "x" else (T.w1, T.w1_in)
+        q.dma_start(dst[:, TW * i:TW * i + TW], src[:, TW * i:TW * i + TW]).then_inc(S["l%s_%d" % (what, i)], 16)
 
     def quant_x(m):
-        g.vector.wait_ge(S["lx%d" % m], 16)
+        g.vector.wait_ge(S["lx_%d" % m], 16)
         g.vector.quantize_mx(T.xq[:, NC * m:NC * m + NC], T.xs[:, NC * m:NC * m + NC],
                              T.x_in[:, TW * m:TW * m + TW]).then_inc(S["qx%d" % m], 1)
+
+    def quant_w1(i):
+        g.vector.wait_ge(S["lw1_%d" % i], 16)
+        g.vector.quantize_mx(T.w1q[:, NC * i:NC * i + NC], T.w1s[:, NC * i:NC * i + NC],
+                             T.w1_in[:, TW * i:TW * i + TW]).then_inc(S["qw%d" % i], 1)
 
     def quant_h(m):
         g.vector.quantize_mx(T.hq[:, NC * m:NC * m + NC], T.hs[:, NC * m:NC * m + NC],
@@ -120,25 +140,21 @@ def rank_program(g, core, T, topo):
                                AluOpType.max, AluOpType.mult).then_inc(S.actv, 1)
 
     if root:
-        load_x(g.sync, 0)
-        for i in range(G):
-            load_w1(g.sync if i % 2 else g.scalar, i)
-        load_x(g.scalar, 1)
+        for k in range(len(LOADS)):
+            load(k)
     if rank is not None:
         g.sync.dma_start(T.w2_in[:], T.w2[:]).then_inc(S.lv, 16)
     if root:
         quant_x(0)
         g.tensor.wait_ge(S.qx0, 1)
         for i in range(G):
-            a, b = NC * i, NC * i + NC
-            g.vector.wait_ge(S["lw%d" % i], 16)
-            g.vector.quantize_mx(T.w1q[:, a:b], T.w1s[:, a:b], T.w1_in[:, TW * i:TW * i + TW]).then_inc(S["qw%d" % i], 1)
+            quant_w1(i)
             g.tensor.wait_ge(S["qw%d" % i], 1)
             product(i, 0)
             relu_scalar(i, 0)
+        quant_x(1)
         g.vector.wait_ge(S.act0, G)
         quant_h(0)
-        quant_x(1)
         g.tensor.wait_ge(S.qx1, 1)
         for i in range(G):
             if i == 2:
@@ -153,42 +169,39 @@ def rank_program(g, core, T, topo):
         g.vector.quantize_mx(T.w2q[:], T.w2s[:], T.w2_in[:]).then_inc(S.qv, 1)
 
     total = 0
-    for call in calls.get(core, []):
-        trs = []
-        for p, dsts, pick in call:
-            if root:
-                g.wait_ge(S.qh0 if p == C0 else S.qh1, 1)
-            else:
-                g.wait_ge(S[piece_sem(p)], landing[p])
-            eng = engines(topo, core, dsts, pick)
-            total += len(eng)
-            ids = [DstId(rid=topo.addr(d)[0], pnc=topo.addr(d)[1]) for d in dsts]
-            trs.append(RemoteDMATransfer(dst_ids=ids, dma_engine_mask=sum(1 << b for b in eng),
-                                         remote_sem=S[piece_sem(p)], srcs=[view(T, p)],
-                                         dsts=[view(T, p) for d in dsts]))
-        g.remote_dma_fused(trs, local_sem=S.sent)
+    for p, dsts in calls.get(core, []):
+        if root:
+            g.wait_ge(S["qh%d" % (p[1] // NC)], 1)
+        else:
+            g.wait_ge(S[piece_sem(p)], landing[p])
+        mask = engine_mask(topo, core, calls[core])
+        total += mask.bit_count()
+        ids = [DstId(rid=topo.addr(d)[0], pnc=topo.addr(d)[1]) for d in dsts]
+        g.remote_dma_fused([RemoteDMATransfer(dst_ids=ids, dma_engine_mask=mask, remote_sem=S[piece_sem(p)],
+                                              srcs=[view(T, p)], dsts=[view(T, p) for d in dsts])], local_sem=S.sent)
     if total:
         g.wait_ge(S.sent, total)
 
     if rank is not None:
         g.tensor.wait_ge(S.qv, 1)
-        waited = set()
         for m in range(MB):
             a, b = NC * m, NC * m + NC
             if root:
                 g.tensor.wait_ge(S["qh%d" % m], 1)
             for p in PIECES:
-                if p in landing and p not in waited and p[1] < b and p[2] > a:
-                    waited.add(p)
+                if p in landing and p[1] == a:
                     g.tensor.wait_ge(S[piece_sem(p)], landing[p])
             g.tensor.matmul_mx(T.yp[:, 512 * m:512 * m + NC], T.w2q[:], T.w2s[:], T.hq[:, a:b], T.hs[:, a:b],
                                True, True).then_inc(S["ym%d" % m], 1)
         g.scalar.wait_ge(S.ym0, 1)
         g.scalar.activation(T.ysb[:, 0:NC], T.yp[:, 0:NC], ActivationFunctionType.Copy).then_inc(S.ya, 1)
-        g.scalar.wait_ge(S.ya, 1)
-        g.scalar.dma_start(T.y[:, 0:NC], T.ysb[:, 0:NC]).then_inc(S.sta, 16)
         g.vector.wait_ge(S.ym1, 1)
         g.vector.tensor_copy(T.ysb[:, NC:W], T.yp[:, 512:512 + NC]).then_inc(S.yv, 1)
+        if total:
+            g.scalar.wait_ge(S.sent, total)
+            g.sync.wait_ge(S.sent, total)
+        g.scalar.wait_ge(S.ya, 1)
+        g.scalar.dma_start(T.y[:, 0:NC], T.ysb[:, 0:NC]).then_inc(S.sta, 16)
         g.sync.wait_ge(S.yv, 1)
         g.sync.dma_start(T.y[:, NC:W], T.ysb[:, NC:W]).then_inc(S.stv, 16)
         g.scalar.wait_ge(S.sta, 16)

from concourse.bass import DstId, RemoteDMATransfer
from concourse.mybir import dt, AluOpType, ActivationFunctionType

NC, G, MB = 128, 4, 2
W = NC * MB
TW = 4 * NC
C = 0.043
SIM_CORES = 80

SCRATCH = {
    "x_in": ("sbuf", [128, MB * TW], "bfloat16"),
    "w1_in": ("sbuf", [128, G * TW], "bfloat16"),
    "w2_in": ("sbuf", [128, TW], "bfloat16"),
    "xq": ("sbuf", [128, W], "float8_e4m3fn_x4"),
    "xs": ("sbuf", [128, W], "uint8"),
    "w1q": ("sbuf", [128, G * NC], "float8_e4m3fn_x4"),
    "w1s": ("sbuf", [128, G * NC], "uint8"),
    "w2q": ("sbuf", [128, NC], "float8_e4m3fn_x4"),
    "w2s": ("sbuf", [128, NC], "uint8"),
    "h": ("sbuf", [128, MB * TW], "bfloat16"),
    "hq": ("sbuf", [128, W], "float8_e4m3fn_x4"),
    "hs": ("sbuf", [128, W], "uint8"),
    "ysb": ("sbuf", [128, W], "float32"),
    "z": ("psum", [128, 512 * (G + 2)], "float32"),
    "yp": ("psum", [128, 512 * MB], "float32"),
}
C0, C1, S0, S1 = ("c", 0, NC), ("c", NC, W), ("s", 0, NC), ("s", NC, W)
PIECES = [S0, C0, S1, C1]
BY_CHIP = (S0, C1)
LOADS = [("x", 0), ("w1", 0), ("w1", 1), ("w1", 2), ("w1", 3), ("x", 1)]


def piece_sem(p):
    return "%s%d_%d" % p


SEMAPHORES = (["lv", "qv", "act0", "act1", "actv", "sent", "ya", "yv", "sta", "stv"]
              + ["l%s_%d" % l for l in LOADS] + ["qx%d" % m for m in range(MB)]
              + ["qh%d" % m for m in range(MB)] + ["ym%d" % m for m in range(MB)]
              + ["qw%d" % i for i in range(G)]
              + ["z%d_%d" % (i, m) for i in range(G) for m in range(MB)]
              + [piece_sem(p) for p in PIECES])


def plan(T, topo):
    root = T.cores[T.root]
    home = topo.chip(root)
    far = [c for c in T.cores if c != root and not topo.may_write(root, c)]
    near = [c for c in T.cores if c != root and topo.may_write(root, c)]

    def owners(ok):
        cs = [c for c in range(SIM_CORES) if c != root and topo.may_write(root, c) and ok(topo.chip(c))
              and all(topo.may_write(c, d) for d in far)]
        return sorted(cs, key=lambda c: (c not in near, c))

    by_die, by_chip = [], []
    for die in sorted({topo.die(d) for d in far}):
        relay = [c for c in owners(lambda k: k == home) if topo.die(c) == die][0]
        ranks = [d for d in far if topo.die(d) == die]
        ranks.sort(key=lambda d: topo.mates(topo.chip(d), home))
        by_die.append((relay, ranks))
    taken = [r for r, ranks in by_die]
    for chip in sorted({topo.chip(d) for d in far}, key=lambda k: topo.mates(k, home)):
        free = [c for c in owners(lambda k: topo.mates(k, chip)) if c not in taken]
        want = topo.die(near[0]) if topo.mates(chip, home) else topo.die(root)
        by_chip.append(([c for c in free if topo.die(c) == want][0], [d for d in far if topo.chip(d) == chip]))
    calls = {root: []}
    for p in PIECES:
        relays = by_chip if p in BY_CHIP else by_die
        calls[root].append((p, [r for r, ranks in relays]))
        for r, ranks in relays:
            calls.setdefault(r, []).append((p, ranks))
    for p in PIECES:
        rest = [c for c in near if all(c not in dsts for q, dsts in calls[root] if q == p)]
        if rest:
            calls[root].append((p, rest))
    return calls


def view(T, p):
    k, lo, hi = p
    return T.hq[:, lo:hi].bitcast(dt.uint8) if k == "c" else T.hs[:, lo:hi]


def engine_mask(topo, src, cs):
    m = -1
    for p, dsts in cs:
        for d in dsts:
            m &= topo.mask(src, d)
    return m


def rank_program(g, core, T, topo):
    rank = T.rank_of(core)
    calls = plan(T, topo)
    S = T.sem
    landing = {p: engine_mask(topo, src, cs).bit_count()
               for src, cs in calls.items() for p, dsts in cs if core in dsts}
    root = rank == T.root

    def load(k):
        what, i = LOADS[k]
        q = g.scalar if k % 2 else g.sync
        src, dst = (T.x, T.x_in) if what == "x" else (T.w1, T.w1_in)
        q.dma_start(dst[:, TW * i:TW * i + TW], src[:, TW * i:TW * i + TW]).then_inc(S["l%s_%d" % (what, i)], 16)

    def quant_x(m):
        g.vector.wait_ge(S["lx_%d" % m], 16)
        g.vector.quantize_mx(T.xq[:, NC * m:NC * m + NC], T.xs[:, NC * m:NC * m + NC],
                             T.x_in[:, TW * m:TW * m + TW]).then_inc(S["qx%d" % m], 1)

    def quant_w1(i):
        g.vector.wait_ge(S["lw1_%d" % i], 16)
        g.vector.quantize_mx(T.w1q[:, NC * i:NC * i + NC], T.w1s[:, NC * i:NC * i + NC],
                             T.w1_in[:, TW * i:TW * i + TW]).then_inc(S["qw%d" % i], 1)

    def quant_h(m):
        g.vector.quantize_mx(T.hq[:, NC * m:NC * m + NC], T.hs[:, NC * m:NC * m + NC],
                             T.h[:, TW * m:TW * m + TW]).then_inc(S["qh%d" % m], 1)

    def bank(i, m):
        return 512 * (i if m == 0 else (G + i) % (G + 2))

    def z(i, m):
        return T.z[:, bank(i, m):bank(i, m) + NC]

    def product(i, m):
        a, b, c, d = NC * i, NC * i + NC, NC * m, NC * m + NC
        g.tensor.matmul_mx(z(i, m), T.w1q[:, a:b], T.w1s[:, a:b], T.xq[:, c:d], T.xs[:, c:d],
                           True, True).then_inc(S["z%d_%d" % (i, m)], 1)

    def relu_scalar(i, m):
        g.scalar.wait_ge(S["z%d_%d" % (i, m)], 1)
        g.scalar.activation(T.h[:, TW * m + i:TW * m + TW:G], z(i, m), ActivationFunctionType.Relu,
                            scale=C).then_inc(S["act%d" % m], 1)

    def relu_vector(i, m):
        g.vector.wait_ge(S["z%d_%d" % (i, m)], 1)
        g.vector.tensor_scalar(T.h[:, TW * m + i:TW * m + TW:G], z(i, m), 0.0, C,
                               AluOpType.max, AluOpType.mult).then_inc(S.actv, 1)

    if root:
        for k in range(len(LOADS)):
            load(k)
    if rank is not None:
        g.sync.dma_start(T.w2_in[:], T.w2[:]).then_inc(S.lv, 16)
    if root:
        quant_x(0)
        g.tensor.wait_ge(S.qx0, 1)
        for i in range(G):
            quant_w1(i)
            g.tensor.wait_ge(S["qw%d" % i], 1)
            product(i, 0)
            relu_scalar(i, 0)
        quant_x(1)
        g.vector.wait_ge(S.act0, G)
        quant_h(0)
        g.tensor.wait_ge(S.qx1, 1)
        for i in range(G):
            if i == 2:
                g.tensor.wait_ge(S.act0, G)
            product(i, 1)
            (relu_vector if i % 2 else relu_scalar)(i, 1)
        g.vector.wait_ge(S.act1, G // 2)
        g.vector.wait_ge(S.actv, G // 2)
        quant_h(1)
    if rank is not None:
        g.vector.wait_ge(S.lv, 16)
        g.vector.quantize_mx(T.w2q[:], T.w2s[:], T.w2_in[:]).then_inc(S.qv, 1)

    total = 0
    for p, dsts in calls.get(core, []):
        if root:
            g.wait_ge(S["qh%d" % (p[1] // NC)], 1)
        else:
            g.wait_ge(S[piece_sem(p)], landing[p])
        mask = engine_mask(topo, core, calls[core])
        total += mask.bit_count()
        ids = [DstId(rid=topo.addr(d)[0], pnc=topo.addr(d)[1]) for d in dsts]
        g.remote_dma_fused([RemoteDMATransfer(dst_ids=ids, dma_engine_mask=mask, remote_sem=S[piece_sem(p)],
                                              srcs=[view(T, p)], dsts=[view(T, p) for d in dsts])], local_sem=S.sent)
    if total:
        g.wait_ge(S.sent, total)

    if rank is not None:
        g.tensor.wait_ge(S.qv, 1)
        for m in range(MB):
            a, b = NC * m, NC * m + NC
            if root:
                g.tensor.wait_ge(S["qh%d" % m], 1)
            for p in PIECES:
                if p in landing and p[1] == a:
                    g.tensor.wait_ge(S[piece_sem(p)], landing[p])
            g.tensor.matmul_mx(T.yp[:, 512 * m:512 * m + NC], T.w2q[:], T.w2s[:], T.hq[:, a:b], T.hs[:, a:b],
                               True, True).then_inc(S["ym%d" % m], 1)
        g.scalar.wait_ge(S.ym0, 1)
        g.scalar.activation(T.ysb[:, 0:NC], T.yp[:, 0:NC], ActivationFunctionType.Copy).then_inc(S.ya, 1)
        g.vector.wait_ge(S.ym1, 1)
        g.vector.tensor_copy(T.ysb[:, NC:W], T.yp[:, 512:512 + NC]).then_inc(S.yv, 1)
        if total:
            g.scalar.wait_ge(S.sent, total)
            g.sync.wait_ge(S.sent, total)
        g.scalar.wait_ge(S.ya, 1)
        g.scalar.dma_start(T.y[:, 0:NC], T.ysb[:, 0:NC]).then_inc(S.sta, 16)
        g.sync.wait_ge(S.yv, 1)
        g.sync.dma_start(T.y[:, NC:W], T.ysb[:, NC:W]).then_inc(S.stv, 16)
        g.scalar.wait_ge(S.sta, 16)
        g.sync.wait_ge(S.stv, 16)
